import numpy as np
import ml_dtypes


def mxq(x, axis, fmt="e4m3"):
    dtype, down = {"e4m3": (ml_dtypes.float8_e4m3fn, 7), "e5m2": (ml_dtypes.float8_e5m2, 14)}[fmt]
    v = np.moveaxis(np.asarray(x, np.float32).astype(ml_dtypes.bfloat16).astype(np.float64), axis, -1)
    blocks = v.reshape(v.shape[:-1] + (-1, 32))
    amax = np.abs(blocks).max(-1, keepdims=True)
    byte = np.maximum(np.where(amax > 0, np.frexp(amax)[1] - 1 + 127, 0) - down, 1)
    scale = np.exp2(byte - 127.0)
    codes = (blocks / scale).astype(np.float32).astype(dtype).astype(np.float64)
    return np.moveaxis((codes * scale).reshape(v.shape), -1, axis)


WIDE = False


def mx_kscale(k):
    if not WIDE:
        return np.ones(k)
    levels = np.array([10, -10, 5, -5, 0])
    if k % 512:
        return np.exp2(np.random.permutation(np.resize(levels, k // 32))).repeat(32)
    a = np.empty((k // 512, 16))
    for p in range(k // 512):
        a[p, :8] = np.random.permutation(np.resize(levels, 8))
        for g in range(8):
            far = levels[np.abs(levels - a[p, g]) >= 10]
            a[p, g + 8] = far[np.random.randint(len(far))]
    return np.exp2(a.ravel()).repeat(32)


def f64(x):
    return np.asarray(x).astype(np.float64)


def striped(idx):
    return np.tile(np.asarray(idx).reshape(-1, 16).T, (8, 1)).astype(np.uint16)


def unstriped(offs):
    return offs[:16].T.reshape(-1).astype(np.int64)


def striped8(idx):
    return np.asarray(idx).reshape(8, -1, 16).transpose(0, 2, 1).reshape(128, -1).astype(np.uint16)


def unstriped8(offs):
    return offs.reshape(8, 16, -1).transpose(0, 2, 1).reshape(8, -1).astype(np.int64)


def pick8(x, idx, run):
    r = np.arange(len(x))
    return x[r[:, None], idx[r % (8 * run) // run]]


E2M1 = np.array([0.0, 0.5, 1.0, 1.5, 2.0, 3.0, 4.0, 6.0, -0.0, -0.5, -1.0, -1.5, -2.0, -3.0, -4.0, -6.0])


def pack_weight(w, fmt):
    k, n = w.shape
    w = f64(np.asarray(w, np.float32).astype(ml_dtypes.bfloat16)).reshape(k // 32, 32, n)
    amax = np.abs(w).max(1)
    if fmt == "e4m3":
        byte = np.frexp(amax)[1] - 1 + 127 - 7
    else:
        mant, ex = np.frexp(amax / 6.0)
        byte = np.where(mant > 0.5, ex, ex - 1) + 127
    byte = np.clip(np.where(amax > 0, byte, 1), 1, 254)
    scaled = (w * np.exp2(127.0 - byte)[:, None, :]).reshape(k, n).astype(np.float32)
    by_word = np.ascontiguousarray(scaled.reshape(k // 512, 128, 4, n).transpose(0, 1, 3, 2))
    if fmt == "e4m3":
        words = by_word.astype(ml_dtypes.float8_e4m3fn).view(np.uint8)
    else:
        c = by_word.astype(ml_dtypes.float4_e2m1fn).view(np.uint8) & 0xF
        words = (c[..., 0::2] | (c[..., 1::2] << 4)).reshape(k // 512, 128, 2 * n)
    return np.ascontiguousarray(words), np.ascontiguousarray(byte.astype(np.uint8).reshape(k // 512, 16, n))


def unpack_weight(words, scales, fmt):
    g, _, n = scales.shape
    words = np.ascontiguousarray(words).reshape(g, 128, n, -1)
    if fmt == "e4m3":
        vals = words.view(ml_dtypes.float8_e4m3fn).astype(np.float64)
    else:
        nib = np.empty((g, 128, n, 4), np.uint8)
        nib[..., 0::2] = words & 0xF
        nib[..., 1::2] = words >> 4
        vals = E2M1[nib]
    vals = vals * np.repeat(np.exp2(scales.astype(np.float64) - 127.0), 8, axis=1)[..., None]
    return vals.transpose(0, 1, 3, 2).reshape(g * 512, n)


K, J, R, T, U, Z, M, O, N, S = 512, 256, 512, 512, 512, 512, 1024, 128, 256, 1024


def setup_inputs():
    n = np.random.standard_normal
    idx = np.stack([np.random.permutation(T)[:J] for _ in range(8)])
    idx2 = np.stack([np.random.permutation(U)[:J] for _ in range(8)])
    idx3 = np.stack([np.random.permutation(U)[:J] for _ in range(8)])
    idx4 = np.random.permutation(M)[:J]
    idx5 = np.stack([np.random.permutation(J)[:O] for _ in range(8)])
    idx6 = np.stack([np.random.permutation(J)[:O] for _ in range(8)])
    idx7 = np.random.permutation(S)[:N]
    fk = mx_kscale(K)
    fr = mx_kscale(R)
    fz = mx_kscale(Z)
    wp = pack_weight(n((K, R)) * 1 / np.sqrt(K) / fk[:, None] * fr, "e2m1")
    xop = pack_weight(n((Z, M)) / fz[:, None], "e2m1")
    w2p = pack_weight(n((Z, R)) * 1 / np.sqrt(Z) * fz[:, None] * fr, "e4m3")
    vsp = pack_weight(n((R, S)) * 1 / np.sqrt(R) / fr[:, None], "e4m3")
    return {
        "ta": (np.random.randint(-7, 8, (K, T)).astype(np.float64)).astype(np.float32),
        "ga": ((np.random.randint(8, 25, (K, 1)) / 64.0) * fk[:, None]).astype(np.float32),
        "gb": (np.random.uniform(0.5, 1.6, (K, 1))).astype(np.float32),
        "w_words": wp[0],
        "w_scales": wp[1],
        "xo_words": xop[0],
        "xo_scales": xop[1],
        "w2_words": w2p[0],
        "w2_scales": w2p[1],
        "sa": (np.random.uniform(0.5, 1.6, (R, 1))).astype(np.float32),
        "sb": (np.random.uniform(0.5, 1.6, (R, 1))).astype(np.float32),
        "vs_words": vsp[0],
        "vs_scales": vsp[1],
        "offs": striped8(idx),
        "offs2": striped8(idx2),
        "offs3": striped8(idx3),
        "offs4": striped(idx4),
        "offs5": striped8(idx5),
        "offs6": striped8(idx6),
        "offs7": striped(idx7),
    }


def reference(ta, ga, gb, w_words, w_scales, xo_words, xo_scales, w2_words, w2_scales, sa, sb, vs_words, vs_scales, offs, offs2, offs3, offs4, offs5, offs6, offs7):
    idx = unstriped8(offs)
    idx2 = unstriped8(offs2)
    idx3 = unstriped8(offs3)
    idx4 = unstriped(offs4)
    idx5 = unstriped8(offs5)
    idx6 = unstriped8(offs6)
    idx7 = unstriped(offs7)
    wu = unpack_weight(w_words, w_scales, "e2m1")
    xou = unpack_weight(xo_words, xo_scales, "e2m1")
    w2u = unpack_weight(w2_words, w2_scales, "e4m3")
    vsu = unpack_weight(vs_words, vs_scales, "e4m3")
    xcd = pick8(f64(ta), idx, 64) * f64(ga)
    xcp = np.zeros((K, U))
    xcp[np.arange(K)[:, None], idx2[np.arange(K) % 512 // 64]] = xcd
    xc = pick8(xcp, idx3, 64) * f64(gb)
    xcq = mxq(xc, 0, "e4m3")
    xoidx4g = xou[:, idx4]
    a = wu.T @ xcq + w2u.T @ xoidx4g
    hid = np.maximum(pick8(a, idx5, 64) * f64(sa), pick8(a, idx6, 64) * f64(sb))
    vsidx7g = vsu[:, idx7]
    hidq = mxq(hid, 0, "e4m3")
    y = vsidx7g.T @ hidq
    return y

@@ -1,0 +1,209 @@
+from contextlib import ExitStack
+
+import concourse.mybir as mybir
+
+K, J, R, T, U, Z, M, O, N, S = 512, 256, 512, 512, 512, 512, 1024, 128, 256, 1024
+FLOPS = 2 * (K * R * J + Z * R * J + R * N * O)
+
+F32 = mybir.dt.float32
+BF16 = mybir.dt.bfloat16
+I32 = mybir.dt.int32
+U32 = mybir.dt.uint32
+U16 = mybir.dt.uint16
+U8 = mybir.dt.uint8
+FP8X4 = mybir.dt.float8_e4m3fn_x4
+FP4X4 = mybir.dt.float4_e2m1fn_x4
+COPY = mybir.ActivationFunctionType.Copy
+MAX = mybir.AluOpType.max
+
+P = 128
+PACK = 4
+QUADS = 4
+
+
+def tile_picked_codepage_plain_bank_grouppair_store_plain_kernel(
+    tc, ta, ga, gb, w_words, w_scales, xo_words, xo_scales, w2_words, w2_scales, sa, sb,
+    vs_words, vs_scales, offs, offs2, offs3, offs4, offs5, offs6, offs7, out,
+):
+    nc = tc.nc
+    with ExitStack() as ctx:
+        lists = ctx.enter_context(tc.tile_pool(name="lists", bufs=1))
+        sbuf = ctx.enter_context(tc.tile_pool(name="sbuf", bufs=1))
+        psum = ctx.enter_context(tc.psum_pool(name="psum", bufs=1))
+
+        def load_list(name, src):
+            tile = lists.tile(list(src.shape), U16, name=name)
+            nc.sync.dma_start(tile[:], src)
+            return tile
+
+        def load_column(name, src, queue):
+            tile = sbuf.tile([P, PACK], F32, name=name)
+            queue.dma_start(tile[:], src.rearrange("(p t) one -> p (t one)", t=PACK))
+            return tile
+
+        def load_ta(t):
+            tile = sbuf.tile([P, T], F32, name="ta%d" % t, tag="ta%d" % t, align_bytes=64)
+            nc.sync.dma_start(tile[:], ta.rearrange("(p t) c -> p t c", t=PACK)[:, t, :])
+            return tile
+
+        def load_words(name, src, width, dtype):
+            tile = sbuf.tile([P, width], dtype, name=name, tag=name, align_bytes=64)
+            nc.sync.dma_start(tile[:].bitcast(I32), src.bitcast(I32))
+            return tile
+
+        def load_scales(dst, src):
+            for q in range(QUADS):
+                nc.sync.dma_start(dst[32 * q : 32 * q + 4, :].bitcast(I32), src[0, 4 * q : 4 * q + 4, :].bitcast(I32))
+
+        staged = sbuf.tile([P, R], U8, name="staged")
+        nc.vector.memset(staged[32:64, :].bitcast(I32), 0)
+        nc.vector.memset(staged[64:128, :].bitcast(I32), 0)
+        xo_sc = sbuf.tile([P, M], U8, name="xo_sc")
+        nc.gpsimd.memset(xo_sc[:].bitcast(I32), 0)
+        planes = sbuf.tile([P, 2, R + J], U8, name="planes", align_bytes=64)
+        vs_sc = sbuf.tile([P, S], U8, name="vs_sc", align_bytes=64)
+        nc.vector.memset(planes[:].rearrange("p a c -> p (a c)").bitcast(I32), 0)
+        nc.vector.memset(vs_sc[:].bitcast(I32), 0)
+        page = [sbuf.tile([P, U], F32, name="page%d" % t) for t in range(PACK)]
+        for t in range(PACK):
+            nc.gpsimd.memset(page[t][:], 0.0)
+
+        ta_t = [load_ta(0)]
+        l1 = load_list("l1", offs)
+        ga_t = load_column("ga_t", ga, nc.sync)
+        for a, src in enumerate((w_scales, w2_scales)):
+            nc.sync.dma_start(staged[a:32:2, :].bitcast(I32), src[0].bitcast(I32))
+        l4 = load_list("l4", offs4)
+        nc.sync.dma_start(xo_sc[0:32:2, :].bitcast(I32), xo_scales[0].bitcast(I32))
+        l2 = load_list("l2", offs2)
+        ta_t.append(load_ta(1))
+        w_w = load_words("w_w", w_words[0], 2 * R, U8)
+        ta_t.append(load_ta(2))
+        w2_w = load_words("w2_w", w2_words[0].rearrange("p n t -> p (n t)"), R, U32)
+        ta_t.append(load_ta(3))
+        l3 = load_list("l3", offs3)
+        gb_t = load_column("gb_t", gb, nc.sync)
+        xo_w = load_words("xo_w", xo_words[0], M, U16)
+        dealt = sbuf.tile([P, R + J], U8, name="dealt")
+        nc.vector.tensor_copy(
+            dealt[:, 0:R].rearrange("p (t m) -> p t m", t=PACK),
+            staged[:].rearrange("p (m t) -> p t m", t=PACK),
+        )
+        xo_gs = sbuf.tile([P, J], U8, name="xo_gs")
+        nc.vector.tensor_copy(xo_gs[:], xo_sc[:].indirect(l4[:]))
+        nc.vector.tensor_copy(dealt[:, R : R + J].bitcast(I32), xo_gs[:].bitcast(I32))
+        for q in range(QUADS):
+            nc.sync.dma_start(
+                planes[32 * q : 32 * q + 4, :, :].bitcast(I32),
+                dealt[8 * q : 8 * q + 8, :].bitcast(I32),
+            )
+        l7 = load_list("l7", offs7)
+        vs_w = load_words("vs_w", vs_words[0].rearrange("p n t -> p (n t)"), S, U32)
+        load_scales(vs_sc[:], vs_scales)
+        l5 = load_list("l5", offs5)
+        l6 = load_list("l6", offs6)
+        sa_t = load_column("sa_t", sa, nc.sync)
+        sb_t = load_column("sb_t", sb, nc.sync)
+
+        for t in range(PACK):
+            xcd = sbuf.tile([P, J], F32, name="xcd%d" % t, tag="xcd%d" % t, align_bytes=64)
+            nc.scalar.activation(xcd[:], ta_t[t][:].indirect(l1[:]), COPY, scale=ga_t[:, t : t + 1])
+            nc.vector.tensor_copy(page[t][:].indirect(l2[:]), xcd[:])
+
+        w_d = sbuf.tile([P, 2 * R], U8, name="w_d", align_bytes=64)
+        nc.scalar.copy(
+            w_d[:].bitcast(U16).rearrange("p (t m) -> p t m", t=PACK),
+            w_w[:].bitcast(U16).rearrange("p (m t) -> p t m", t=PACK),
+        )
+        w2_d = sbuf.tile([P, R], U32, name="w2_d", align_bytes=64)
+        nc.scalar.copy(
+            w2_d[:].rearrange("p (t m) -> p t m", t=PACK),
+            w2_w[:].rearrange("p (m t) -> p t m", t=PACK),
+        )
+        xo_g = sbuf.tile([P, J], U16, name="xo_g", tag="xcd3", align_bytes=64)
+        nc.vector.tensor_copy(xo_g[:], xo_w[:].indirect(l4[:]))
+
+        xc = sbuf.tile([P, PACK, J], BF16, name="xc", tag="ta3", align_bytes=64)
+        xc_i = sbuf.tile([P, J, PACK], BF16, name="xc_i", tag="xo_w", align_bytes=64)
+        for t in range(PACK - 1):
+            nc.scalar.activation(xc[:, t, :], page[t][:].indirect(l3[:]), COPY, scale=gb_t[:, t : t + 1])
+        t = PACK - 1
+        halves = [slice(0, J // 2), slice(J // 2, J)]
+        for h in halves:
+            nc.scalar.activation(
+                xc[:, t, h], page[t][:].indirect(l3[:, h.start // 16 : h.stop // 16]), COPY, scale=gb_t[:, t : t + 1]
+            )
+            nc.vector.tensor_copy(xc_i[:, h, :], xc[:, :, h].rearrange("p t j -> p j t"))
+        xc_q = sbuf.tile([P, J], U32, name="xc_q", tag="xc_q", align_bytes=64)
+        xc_s = sbuf.tile([P, J], U8, name="xc_s", align_bytes=64)
+        for h in halves:
+            nc.vector.quantize_mx(
+                out=xc_q[:, h].bitcast(FP8X4), scales=xc_s[:, h], in_=xc_i[:, h, :].rearrange("p j t -> p (j t)")
+            )
+
+        acc = [psum.tile([P, J], F32, name="acc%d" % t) for t in range(PACK)]
+        for t in range(PACK):
+            nc.tensor.matmul_mx(
+                out=acc[t][:],
+                lhsT=w2_d[:, P * t : P * (t + 1)].bitcast(FP8X4),
+                lhsT_scale=planes[:, 1, P * t : P * (t + 1)],
+                rhs=xo_g[:].bitcast(FP4X4),
+                rhs_scale=planes[:, 0, R : R + J],
+                start=True,
+                stop=False,
+            )
+        for t in range(PACK):
+            nc.tensor.matmul_mx(
+                out=acc[t][:],
+                lhsT=w_d[:, 2 * P * t : 2 * P * (t + 1)].bitcast(FP4X4),
+                lhsT_scale=planes[:, 0, P * t : P * (t + 1)],
+                rhs=xc_q[:].bitcast(FP8X4),
+                rhs_scale=xc_s[:],
+                start=False,
+                stop=True,
+            )
+
+        first = [sbuf.tile([P, 2, O], F32, name="first%d" % h) for h in range(2)]
+        second = [sbuf.tile([P, 2, O], F32, name="second%d" % h) for h in range(2)]
+        hid_i = sbuf.tile([P, O, PACK], BF16, name="hid_i", align_bytes=64)
+        vs_g = sbuf.tile([P, N], U32, name="vs_g", tag="xo_w", align_bytes=64)
+        nc.vector.tensor_copy(vs_g[:], vs_w[:].indirect(l7[:]))
+        vs_gs = sbuf.tile([P, N], U8, name="vs_gs", tag="xc_q", align_bytes=64)
+        for t in range(PACK):
+            a_t = sbuf.tile([P, J], F32, name="a%d" % t)
+            if t == 0:
+                nc.scalar.copy(a_t[:], acc[t][:])
+            else:
+                nc.vector.tensor_copy(a_t[:], acc[t][:])
+            nc.scalar.activation(first[t // 2][:, t % 2, :], a_t[:].indirect(l5[:]), COPY, scale=sa_t[:, t : t + 1])
+            nc.scalar.activation(second[t // 2][:, t % 2, :], a_t[:].indirect(l6[:]), COPY, scale=sb_t[:, t : t + 1])
+        nc.vector.tensor_copy(vs_gs[:], vs_sc[:].indirect(l7[:]))
+        for h in range(2):
+            nc.vector.tensor_tensor(
+                hid_i[:, :, 2 * h : 2 * h + 2],
+                first[h][:].rearrange("p t o -> p o t"),
+                second[h][:].rearrange("p t o -> p o t"),
+                MAX,
+            )
+        hid_q = sbuf.tile([P, O], U32, name="hid_q", align_bytes=64)
+        hid_s = sbuf.tile([P, O], U8, name="hid_s", align_bytes=64)
+        nc.vector.quantize_mx(out=hid_q[:].bitcast(FP8X4), scales=hid_s[:], in_=hid_i[:].rearrange("p o t -> p (o t)"))
+
+        for h in range(N // P):
+            y = psum.tile([P, O], F32, name="y%d" % h)
+            nc.tensor.matmul_mx(
+                out=y[:],
+                lhsT=vs_g[:, P * h : P * (h + 1)].bitcast(FP8X4),
+                lhsT_scale=vs_gs[:, P * h : P * (h + 1)],
+                rhs=hid_q[:].bitcast(FP8X4),
+                rhs_scale=hid_s[:],
+                start=True,
+                stop=True,
+            )
+            res = sbuf.tile([P, O], F32, name="res%d" % h)
+            if h == 0:
+                nc.vector.tensor_copy(res[:], y[:])
+                nc.sync.dma_start(out[P * h : P * (h + 1), :], res[:])
+            else:
+                nc.scalar.copy(res[:], y[:])
+                nc.scalar.dma_start(out[P * h : P * (h + 1), :], res[:])

@@ -55,6 +55,10 @@ def tile_picked_codepage_plain_bank_grouppair_store_plain_kernel(
             for q in range(QUADS):
                 nc.sync.dma_start(dst[32 * q : 32 * q + 4, :].bitcast(I32), src[0, 4 * q : 4 * q + 4, :].bitcast(I32))
 
+        warm_in = sbuf.tile([P, 1], F32, name="warm_in")
+        warm_out = sbuf.tile([P, 1], F32, name="warm_out")
+        nc.gpsimd.memset(warm_in[:], 0.0)
+        nc.scalar.activation(warm_out[:], warm_in[:], COPY)
         staged = sbuf.tile([P, R], U8, name="staged")
         nc.vector.memset(staged[32:64, :].bitcast(I32), 0)
         nc.vector.memset(staged[64:128, :].bitcast(I32), 0)

@@ -29,6 +29,7 @@ def tile_picked_codepage_plain_bank_grouppair_store_plain_kernel(
     with ExitStack() as ctx:
         lists = ctx.enter_context(tc.tile_pool(name="lists", bufs=1))
         sbuf = ctx.enter_context(tc.tile_pool(name="sbuf", bufs=1))
+        late = ctx.enter_context(tc.tile_pool(name="late", bufs=1))
         psum = ctx.enter_context(tc.psum_pool(name="psum", bufs=1))
 
         def load_list(name, src):
@@ -36,9 +37,8 @@ def tile_picked_codepage_plain_bank_grouppair_store_plain_kernel(
             nc.sync.dma_start(tile[:], src)
             return tile
 
-        def load_column(name, src, queue):
-            tile = sbuf.tile([P, PACK], F32, name=name)
-            queue.dma_start(tile[:], src.rearrange("(p t) one -> p (t one)", t=PACK))
+        def load_column(tile, src):
+            nc.sync.dma_start(tile[:], src.rearrange("(p t) one -> p (t one)", t=PACK))
             return tile
 
         def load_ta(t):
@@ -56,27 +56,23 @@ def tile_picked_codepage_plain_bank_grouppair_store_plain_kernel(
                 nc.sync.dma_start(dst[32 * q : 32 * q + 4, :].bitcast(I32), src[0, 4 * q : 4 * q + 4, :].bitcast(I32))
 
         warm_in = sbuf.tile([P, 1], F32, name="warm_in")
-        warm_out = sbuf.tile([P, 1], F32, name="warm_out")
-        nc.gpsimd.memset(warm_in[:], 0.0)
-        nc.scalar.activation(warm_out[:], warm_in[:], COPY)
-        staged = sbuf.tile([P, R], U8, name="staged")
-        nc.vector.memset(staged[32:64, :].bitcast(I32), 0)
-        nc.vector.memset(staged[64:128, :].bitcast(I32), 0)
+        nc.vector.memset(warm_in[:], 0.0)
         xo_sc = sbuf.tile([P, M], U8, name="xo_sc")
         nc.gpsimd.memset(xo_sc[:].bitcast(I32), 0)
-        planes = sbuf.tile([P, 2, R + J], U8, name="planes", align_bytes=64)
-        vs_sc = sbuf.tile([P, S], U8, name="vs_sc", align_bytes=64)
-        nc.vector.memset(planes[:].rearrange("p a c -> p (a c)").bitcast(I32), 0)
-        nc.vector.memset(vs_sc[:].bitcast(I32), 0)
+        staged = sbuf.tile([P, R], U8, name="staged")
+        for lo, hi in ((32, 64), (64, 128)):
+            nc.vector.memset(staged[lo:hi, :].bitcast(I32), 0)
         page = [sbuf.tile([P, U], F32, name="page%d" % t) for t in range(PACK)]
         for t in range(PACK):
-            nc.gpsimd.memset(page[t][:], 0.0)
+            (nc.vector if t < 2 else nc.gpsimd).memset(page[t][:], 0.0)
+        planes = sbuf.tile([P, 2, R + J], U8, name="planes", align_bytes=64)
+        nc.vector.memset(planes[:].rearrange("p a c -> p (a c)").bitcast(I32), 0)
 
+        for a, src in enumerate((w_scales, w2_scales)):
+            nc.scalar.dma_start(staged[a:32:2, :].bitcast(I32), src[0].bitcast(I32))
         ta_t = [load_ta(0)]
         l1 = load_list("l1", offs)
-        ga_t = load_column("ga_t", ga, nc.sync)
-        for a, src in enumerate((w_scales, w2_scales)):
-            nc.sync.dma_start(staged[a:32:2, :].bitcast(I32), src[0].bitcast(I32))
+        ga_t = load_column(sbuf.tile([P, PACK], F32, name="ga_t"), ga)
         l4 = load_list("l4", offs4)
         nc.sync.dma_start(xo_sc[0:32:2, :].bitcast(I32), xo_scales[0].bitcast(I32))
         l2 = load_list("l2", offs2)
@@ -86,14 +82,17 @@ def tile_picked_codepage_plain_bank_grouppair_store_plain_kernel(
         w2_w = load_words("w2_w", w2_words[0].rearrange("p n t -> p (n t)"), R, U32)
         ta_t.append(load_ta(3))
         l3 = load_list("l3", offs3)
-        gb_t = load_column("gb_t", gb, nc.sync)
+        gb_t = load_column(sbuf.tile([P, PACK], F32, name="gb_t"), gb)
         xo_w = load_words("xo_w", xo_words[0], M, U16)
+        l7 = load_list("l7", offs7)
+        l5 = load_list("l5", offs5)
+        l6 = load_list("l6", offs6)
         dealt = sbuf.tile([P, R + J], U8, name="dealt")
         nc.vector.tensor_copy(
             dealt[:, 0:R].rearrange("p (t m) -> p t m", t=PACK),
             staged[:].rearrange("p (m t) -> p t m", t=PACK),
         )
-        xo_gs = sbuf.tile([P, J], U8, name="xo_gs")
+        xo_gs = late.tile([P, J], U8, name="xo_gs", offset=4032, align_bytes=64)
         nc.vector.tensor_copy(xo_gs[:], xo_sc[:].indirect(l4[:]))
         nc.vector.tensor_copy(dealt[:, R : R + J].bitcast(I32), xo_gs[:].bitcast(I32))
         for q in range(QUADS):
@@ -101,14 +100,16 @@ def tile_picked_codepage_plain_bank_grouppair_store_plain_kernel(
                 planes[32 * q : 32 * q + 4, :, :].bitcast(I32),
                 dealt[8 * q : 8 * q + 8, :].bitcast(I32),
             )
-        l7 = load_list("l7", offs7)
-        vs_w = load_words("vs_w", vs_words[0].rearrange("p n t -> p (n t)"), S, U32)
+        vs_w = late.tile([P, S], U32, name="vs_w", offset=0, align_bytes=64)
+        nc.sync.dma_start(vs_w[:].bitcast(I32), vs_words[0].rearrange("p n t -> p (n t)").bitcast(I32))
+        sa_t = load_column(late.tile([P, PACK], F32, name="sa_t", offset=4096), sa)
+        sb_t = load_column(late.tile([P, PACK], F32, name="sb_t", offset=4128), sb)
+        vs_sc = late.tile([P, S], U8, name="vs_sc", offset=4160, align_bytes=64)
+        nc.vector.memset(vs_sc[:].bitcast(I32), 0)
         load_scales(vs_sc[:], vs_scales)
-        l5 = load_list("l5", offs5)
-        l6 = load_list("l6", offs6)
-        sa_t = load_column("sa_t", sa, nc.sync)
-        sb_t = load_column("sb_t", sb, nc.sync)
 
+        warm_out = sbuf.tile([P, 1], F32, name="warm_out")
+        nc.scalar.activation(warm_out[:], warm_in[:], COPY)
         for t in range(PACK):
             xcd = sbuf.tile([P, J], F32, name="xcd%d" % t, tag="xcd%d" % t, align_bytes=64)
             nc.scalar.activation(xcd[:], ta_t[t][:].indirect(l1[:]), COPY, scale=ga_t[:, t : t + 1])
@@ -169,7 +170,7 @@ def tile_picked_codepage_plain_bank_grouppair_store_plain_kernel(
 
         first = [sbuf.tile([P, 2, O], F32, name="first%d" % h) for h in range(2)]
         second = [sbuf.tile([P, 2, O], F32, name="second%d" % h) for h in range(2)]
-        hid_i = sbuf.tile([P, O, PACK], BF16, name="hid_i", align_bytes=64)
+        hid_i = late.tile([P, O, PACK], BF16, name="hid_i", offset=4160, align_bytes=64)
         vs_g = sbuf.tile([P, N], U32, name="vs_g", tag="xo_w", align_bytes=64)
         nc.vector.tensor_copy(vs_g[:], vs_w[:].indirect(l7[:]))
         vs_gs = sbuf.tile([P, N], U8, name="vs_gs", tag="xc_q", align_bytes=64)

from contextlib import ExitStack

import concourse.mybir as mybir

K, J, R, T, U, Z, M, O, N, S = 512, 256, 512, 512, 512, 512, 1024, 128, 256, 1024
FLOPS = 2 * (K * R * J + Z * R * J + R * N * O)

F32 = mybir.dt.float32
BF16 = mybir.dt.bfloat16
I32 = mybir.dt.int32
U32 = mybir.dt.uint32
U16 = mybir.dt.uint16
U8 = mybir.dt.uint8
FP8X4 = mybir.dt.float8_e4m3fn_x4
FP4X4 = mybir.dt.float4_e2m1fn_x4
COPY = mybir.ActivationFunctionType.Copy
MAX = mybir.AluOpType.max

P = 128
PACK = 4
QUADS = 4


def tile_picked_codepage_plain_bank_grouppair_store_plain_kernel(
    tc, ta, ga, gb, w_words, w_scales, xo_words, xo_scales, w2_words, w2_scales, sa, sb,
    vs_words, vs_scales, offs, offs2, offs3, offs4, offs5, offs6, offs7, out,
):
    nc = tc.nc
    with ExitStack() as ctx:
        lists = ctx.enter_context(tc.tile_pool(name="lists", bufs=1))
        sbuf = ctx.enter_context(tc.tile_pool(name="sbuf", bufs=1))
        late = ctx.enter_context(tc.tile_pool(name="late", bufs=1))
        psum = ctx.enter_context(tc.psum_pool(name="psum", bufs=1))

        def load_list(name, src):
            tile = lists.tile(list(src.shape), U16, name=name)
            nc.sync.dma_start(tile[:], src)
            return tile

        def load_column(tile, src):
            nc.sync.dma_start(tile[:], src.rearrange("(p t) one -> p (t one)", t=PACK))
            return tile

        def load_ta(t):
            tile = sbuf.tile([P, T], F32, name="ta%d" % t, tag="ta%d" % t, align_bytes=64)
            nc.sync.dma_start(tile[:], ta.rearrange("(p t) c -> p t c", t=PACK)[:, t, :])
            return tile

        def load_words(name, src, width, dtype):
            tile = sbuf.tile([P, width], dtype, name=name, tag=name, align_bytes=64)
            nc.sync.dma_start(tile[:].bitcast(I32), src.bitcast(I32))
            return tile

        def load_scales(dst, src):
            for q in range(QUADS):
                nc.sync.dma_start(dst[32 * q : 32 * q + 4, :].bitcast(I32), src[0, 4 * q : 4 * q + 4, :].bitcast(I32))

        warm_in = sbuf.tile([P, 1], F32, name="warm_in")
        nc.vector.memset(warm_in[:], 0.0)
        xo_sc = sbuf.tile([P, M], U8, name="xo_sc")
        nc.gpsimd.memset(xo_sc[:].bitcast(I32), 0)
        staged = sbuf.tile([P, R], U8, name="staged")
        for lo, hi in ((32, 64), (64, 128)):
            nc.vector.memset(staged[lo:hi, :].bitcast(I32), 0)
        page = [sbuf.tile([P, U], F32, name="page%d" % t) for t in range(PACK)]
        for t in range(PACK):
            (nc.vector if t < 2 else nc.gpsimd).memset(page[t][:], 0.0)
        planes = sbuf.tile([P, 2, R + J], U8, name="planes", align_bytes=64)
        nc.vector.memset(planes[:].rearrange("p a c -> p (a c)").bitcast(I32), 0)

        for a, src in enumerate((w_scales, w2_scales)):
            nc.scalar.dma_start(staged[a:32:2, :].bitcast(I32), src[0].bitcast(I32))
        ta_t = [load_ta(0)]
        l1 = load_list("l1", offs)
        ga_t = load_column(sbuf.tile([P, PACK], F32, name="ga_t"), ga)
        l4 = load_list("l4", offs4)
        nc.sync.dma_start(xo_sc[0:32:2, :].bitcast(I32), xo_scales[0].bitcast(I32))
        l2 = load_list("l2", offs2)
        ta_t.append(load_ta(1))
        w_w = load_words("w_w", w_words[0], 2 * R, U8)
        ta_t.append(load_ta(2))
        w2_w = load_words("w2_w", w2_words[0].rearrange("p n t -> p (n t)"), R, U32)
        ta_t.append(load_ta(3))
        l3 = load_list("l3", offs3)
        gb_t = load_column(sbuf.tile([P, PACK], F32, name="gb_t"), gb)
        xo_w = load_words("xo_w", xo_words[0], M, U16)
        l7 = load_list("l7", offs7)
        l5 = load_list("l5", offs5)
        l6 = load_list("l6", offs6)
        dealt = sbuf.tile([P, R + J], U8, name="dealt")
        nc.vector.tensor_copy(
            dealt[:, 0:R].rearrange("p (t m) -> p t m", t=PACK),
            staged[:].rearrange("p (m t) -> p t m", t=PACK),
        )
        xo_gs = late.tile([P, J], U8, name="xo_gs", offset=4032, align_bytes=64)
        nc.vector.tensor_copy(xo_gs[:], xo_sc[:].indirect(l4[:]))
        nc.vector.tensor_copy(dealt[:, R : R + J].bitcast(I32), xo_gs[:].bitcast(I32))
        for q in range(QUADS):
            nc.sync.dma_start(
                planes[32 * q : 32 * q + 4, :, :].bitcast(I32),
                dealt[8 * q : 8 * q + 8, :].bitcast(I32),
            )
        vs_w = late.tile([P, S], U32, name="vs_w", offset=0, align_bytes=64)
        nc.sync.dma_start(vs_w[:].bitcast(I32), vs_words[0].rearrange("p n t -> p (n t)").bitcast(I32))
        sa_t = load_column(late.tile([P, PACK], F32, name="sa_t", offset=4096), sa)
        sb_t = load_column(late.tile([P, PACK], F32, name="sb_t", offset=4128), sb)
        vs_sc = late.tile([P, S], U8, name="vs_sc", offset=4160, align_bytes=64)
        nc.vector.memset(vs_sc[:].bitcast(I32), 0)
        load_scales(vs_sc[:], vs_scales)

        warm_out = sbuf.tile([P, 1], F32, name="warm_out")
        nc.scalar.activation(warm_out[:], warm_in[:], COPY)
        for t in range(PACK):
            xcd = sbuf.tile([P, J], F32, name="xcd%d" % t, tag="xcd%d" % t, align_bytes=64)
            nc.scalar.activation(xcd[:], ta_t[t][:].indirect(l1[:]), COPY, scale=ga_t[:, t : t + 1])
            nc.vector.tensor_copy(page[t][:].indirect(l2[:]), xcd[:])

        w_d = sbuf.tile([P, 2 * R], U8, name="w_d", align_bytes=64)
        nc.scalar.copy(
            w_d[:].bitcast(U16).rearrange("p (t m) -> p t m", t=PACK),
            w_w[:].bitcast(U16).rearrange("p (m t) -> p t m", t=PACK),
        )
        w2_d = sbuf.tile([P, R], U32, name="w2_d", align_bytes=64)
        nc.scalar.copy(
            w2_d[:].rearrange("p (t m) -> p t m", t=PACK),
            w2_w[:].rearrange("p (m t) -> p t m", t=PACK),
        )
        xo_g = sbuf.tile([P, J], U16, name="xo_g", tag="xcd3", align_bytes=64)
        nc.vector.tensor_copy(xo_g[:], xo_w[:].indirect(l4[:]))

        xc = sbuf.tile([P, PACK, J], BF16, name="xc", tag="ta3", align_bytes=64)
        xc_i = sbuf.tile([P, J, PACK], BF16, name="xc_i", tag="xo_w", align_bytes=64)
        for t in range(PACK - 1):
            nc.scalar.activation(xc[:, t, :], page[t][:].indirect(l3[:]), COPY, scale=gb_t[:, t : t + 1])
        t = PACK - 1
        halves = [slice(0, J // 2), slice(J // 2, J)]
        for h in halves:
            nc.scalar.activation(
                xc[:, t, h], page[t][:].indirect(l3[:, h.start // 16 : h.stop // 16]), COPY, scale=gb_t[:, t : t + 1]
            )
            nc.vector.tensor_copy(xc_i[:, h, :], xc[:, :, h].rearrange("p t j -> p j t"))
        xc_q = sbuf.tile([P, J], U32, name="xc_q", tag="xc_q", align_bytes=64)
        xc_s = sbuf.tile([P, J], U8, name="xc_s", align_bytes=64)
        for h in halves:
            nc.vector.quantize_mx(
                out=xc_q[:, h].bitcast(FP8X4), scales=xc_s[:, h], in_=xc_i[:, h, :].rearrange("p j t -> p (j t)")
            )

        acc = [psum.tile([P, J], F32, name="acc%d" % t) for t in range(PACK)]
        for t in range(PACK):
            nc.tensor.matmul_mx(
                out=acc[t][:],
                lhsT=w2_d[:, P * t : P * (t + 1)].bitcast(FP8X4),
                lhsT_scale=planes[:, 1, P * t : P * (t + 1)],
                rhs=xo_g[:].bitcast(FP4X4),
                rhs_scale=planes[:, 0, R : R + J],
                start=True,
                stop=False,
            )
        for t in range(PACK):
            nc.tensor.matmul_mx(
                out=acc[t][:],
                lhsT=w_d[:, 2 * P * t : 2 * P * (t + 1)].bitcast(FP4X4),
                lhsT_scale=planes[:, 0, P * t : P * (t + 1)],
                rhs=xc_q[:].bitcast(FP8X4),
                rhs_scale=xc_s[:],
                start=False,
                stop=True,
            )

        first = [sbuf.tile([P, 2, O], F32, name="first%d" % h) for h in range(2)]
        second = [sbuf.tile([P, 2, O], F32, name="second%d" % h) for h in range(2)]
        hid_i = late.tile([P, O, PACK], BF16, name="hid_i", offset=4160, align_bytes=64)
        vs_g = sbuf.tile([P, N], U32, name="vs_g", tag="xo_w", align_bytes=64)
        nc.vector.tensor_copy(vs_g[:], vs_w[:].indirect(l7[:]))
        vs_gs = sbuf.tile([P, N], U8, name="vs_gs", tag="xc_q", align_bytes=64)
        for t in range(PACK):
            a_t = sbuf.tile([P, J], F32, name="a%d" % t)
            if t == 0:
                nc.scalar.copy(a_t[:], acc[t][:])
            else:
                nc.vector.tensor_copy(a_t[:], acc[t][:])
            nc.scalar.activation(first[t // 2][:, t % 2, :], a_t[:].indirect(l5[:]), COPY, scale=sa_t[:, t : t + 1])
            nc.scalar.activation(second[t // 2][:, t % 2, :], a_t[:].indirect(l6[:]), COPY, scale=sb_t[:, t : t + 1])
        nc.vector.tensor_copy(vs_gs[:], vs_sc[:].indirect(l7[:]))
        for h in range(2):
            nc.vector.tensor_tensor(
                hid_i[:, :, 2 * h : 2 * h + 2],
                first[h][:].rearrange("p t o -> p o t"),
                second[h][:].rearrange("p t o -> p o t"),
                MAX,
            )
        hid_q = sbuf.tile([P, O], U32, name="hid_q", align_bytes=64)
        hid_s = sbuf.tile([P, O], U8, name="hid_s", align_bytes=64)
        nc.vector.quantize_mx(out=hid_q[:].bitcast(FP8X4), scales=hid_s[:], in_=hid_i[:].rearrange("p o t -> p (o t)"))

        for h in range(N // P):
            y = psum.tile([P, O], F32, name="y%d" % h)
            nc.tensor.matmul_mx(
                out=y[:],
                lhsT=vs_g[:, P * h : P * (h + 1)].bitcast(FP8X4),
                lhsT_scale=vs_gs[:, P * h : P * (h + 1)],
                rhs=hid_q[:].bitcast(FP8X4),
                rhs_scale=hid_s[:],
                start=True,
                stop=True,
            )
            res = sbuf.tile([P, O], F32, name="res%d" % h)
            if h == 0:
                nc.vector.tensor_copy(res[:], y[:])
                nc.sync.dma_start(out[P * h : P * (h + 1), :], res[:])
            else:
                nc.scalar.copy(res[:], y[:])
                nc.scalar.dma_start(out[P * h : P * (h + 1), :], res[:])
